import numpy as np
import ml_dtypes


def mxq(x, axis, fmt="e4m3"):
    dtype, down = {"e4m3": (ml_dtypes.float8_e4m3fn, 7), "e5m2": (ml_dtypes.float8_e5m2, 14)}[fmt]
    v = np.moveaxis(np.asarray(x, np.float32).astype(ml_dtypes.bfloat16).astype(np.float64), axis, -1)
    blocks = v.reshape(v.shape[:-1] + (-1, 32))
    amax = np.abs(blocks).max(-1, keepdims=True)
    byte = np.maximum(np.where(amax > 0, np.frexp(amax)[1] - 1 + 127, 0) - down, 1)
    scale = np.exp2(byte - 127.0)
    codes = (blocks / scale).astype(np.float32).astype(dtype).astype(np.float64)
    return np.moveaxis((codes * scale).reshape(v.shape), -1, axis)


WIDE = False


def mx_kscale(k):
    if not WIDE:
        return np.ones(k)
    levels = np.array([10, -10, 5, -5, 0])
    if k % 512:
        return np.exp2(np.random.permutation(np.resize(levels, k // 32))).repeat(32)
    a = np.empty((k // 512, 16))
    for p in range(k // 512):
        a[p, :8] = np.random.permutation(np.resize(levels, 8))
        for g in range(8):
            far = levels[np.abs(levels - a[p, g]) >= 10]
            a[p, g + 8] = far[np.random.randint(len(far))]
    return np.exp2(a.ravel()).repeat(32)


def f64(x):
    return np.asarray(x).astype(np.float64)


def striped(idx):
    return np.tile(idx.reshape(-1, 16).T, (8, 1)).astype(np.uint16)


def unstriped(offs):
    return offs[:16].T.reshape(-1).astype(np.int64)


def pack_weight(w):
    k, n = w.shape
    w = f64(np.asarray(w, np.float32).astype(ml_dtypes.bfloat16)).reshape(k // 32, 32, n)
    amax = np.abs(w).max(1)
    byte = np.clip(np.where(amax > 0, np.frexp(amax)[1] - 1 + 127 - 7, 1), 1, 254)
    scaled = (w * np.exp2(127.0 - byte)[:, None, :]).reshape(k, n).astype(np.float32)
    words = np.ascontiguousarray(scaled.reshape(k // 512, 128, 4, n).transpose(0, 1, 3, 2)).astype(ml_dtypes.float8_e4m3fn).view(np.uint8)
    return words, np.ascontiguousarray(byte.astype(np.uint8).reshape(k // 512, 16, n))


def unpack_weight(words, scales):
    g, p, n, _ = words.shape
    vals = np.ascontiguousarray(words).view(ml_dtypes.float8_e4m3fn).astype(np.float64) * np.repeat(np.exp2(scales.astype(np.float64) - 127.0), 8, axis=1)[..., None]
    return vals.transpose(0, 1, 3, 2).reshape(g * 512, n)


K, T, S, N, U = 1024, 2048, 512, 128, 1024


def setup_inputs():
    n = np.random.standard_normal
    s = mx_kscale(K)[:, None]
    packed_w1 = pack_weight(n((K, N)) / np.sqrt(K) / s)
    return {
        "xT": (n((K, T)) * s).astype(np.float32),
        "w1_words": packed_w1[0],
        "w1_scales": packed_w1[1],
        "scale": np.random.uniform(0.5, 1.5, (N, U)).astype(np.float32),
        "offs": striped(np.random.permutation(T)[:S]),
        "task": striped(np.random.permutation(U)[(U * np.random.uniform(0, 1, S) ** 4).astype(np.int64)]),
    }


def reference(xT, w1_words, w1_scales, scale, offs, task):
    xq = mxq(f64(xT)[:, unstriped(offs)], 0, "e4m3")
    y = unpack_weight(w1_words, w1_scales).T @ xq
    g = f64(scale)[:, unstriped(task)]
    return y * g

@@ -1,0 +1,93 @@
+from contextlib import ExitStack
+
+import concourse.mybir as mybir
+
+K, T, S, N, U = 1024, 2048, 512, 128, 1024
+FLOPS = 2 * K * S * N
+
+F32 = mybir.dt.float32
+BF16 = mybir.dt.bfloat16
+I32 = mybir.dt.int32
+U32 = mybir.dt.uint32
+U16 = mybir.dt.uint16
+U8 = mybir.dt.uint8
+FP8X4 = mybir.dt.float8_e4m3fn_x4
+MULT = mybir.AluOpType.mult
+
+P = 128
+PACK = 4
+PASSES = K // (P * PACK)
+GROUP = 16
+HALVES = 2
+HALF = S // HALVES
+QUADRANT = 32
+SCALE_ROWS = 4
+
+
+def tile_picked_none_e_kernel(tc, xT, w1_words, w1_scales, scale, offs, task, out):
+    nc = tc.nc
+    with ExitStack() as ctx:
+        keep = ctx.enter_context(tc.tile_pool(name="keep", bufs=1))
+        psum = ctx.enter_context(tc.psum_pool(name="psum", bufs=1))
+
+        offsets = keep.tile([P, S // GROUP], U16, name="offsets")
+        tasks = keep.tile([P, S // GROUP], U16, name="tasks")
+        planes = [keep.tile([P, T], F32, name="plane%d" % i) for i in range(PASSES * PACK)]
+        w_codes = keep.tile([P, PASSES, N], U32, name="w_codes", align_bytes=64)
+        w_scales = keep.tile([P, PASSES, N], U8, name="w_scales", align_bytes=64)
+        table = keep.tile([P, U], F32, name="table")
+
+        rows = xT.rearrange("(z p j) t -> z j p t", z=PASSES, j=PACK)
+        for i in range(PASSES * PACK):
+            nc.sync.dma_start(out=planes[i][:], in_=rows[i // PACK, i % PACK])
+            if i == 0:
+                nc.sync.dma_start(offsets[:], offs)
+        nc.sync.dma_start(tasks[:], task)
+        nc.sync.dma_start(
+            out=w_codes[:].bitcast(I32),
+            in_=w1_words.rearrange("z p c r -> p z (c r)").bitcast(I32),
+        )
+        nc.sync.dma_start(out=table[:], in_=scale)
+
+        nc.gpsimd.memset(w_scales[:].bitcast(I32), 0)
+        scale_rows = w1_scales.rearrange("z (q r) c -> r q z c", r=SCALE_ROWS)
+        for r in range(SCALE_ROWS):
+            nc.gpsimd.dma_start(
+                out=w_scales[r:P:QUADRANT].bitcast(I32),
+                in_=scale_rows[r].bitcast(I32),
+            )
+
+        def entries(list_tile, h):
+            return list_tile[:, h * HALF // GROUP : (h + 1) * HALF // GROUP]
+
+        acc = [psum.tile([N, HALF], F32, name="acc%d" % h) for h in range(HALVES)]
+        for z in range(PASSES):
+            grouped = [keep.tile([P, HALF, PACK], BF16, name="grouped%d_%d" % (z, h), align_bytes=64) for h in range(HALVES)]
+            for j in range(PACK):
+                for h in range(HALVES):
+                    nc.vector.tensor_copy(grouped[h][:, :, j], planes[z * PACK + j][:].indirect(entries(offsets, h)))
+            for h in range(HALVES):
+                x_codes = keep.tile([P, HALF], U32, name="x_codes%d_%d" % (z, h), align_bytes=64)
+                x_scales = keep.tile([P, HALF], U8, name="x_scales%d_%d" % (z, h), align_bytes=64)
+                nc.vector.quantize_mx(
+                    out=x_codes[:].bitcast(FP8X4),
+                    scales=x_scales[:],
+                    in_=grouped[h][:].rearrange("p n j -> p (n j)"),
+                )
+                nc.tensor.matmul_mx(
+                    out=acc[h][:],
+                    lhsT=w_codes[:, z, :].bitcast(FP8X4),
+                    lhsT_scale=w_scales[:, z, :],
+                    rhs=x_codes[:].bitcast(FP8X4),
+                    rhs_scale=x_scales[:],
+                    start=(z == 0),
+                    stop=(z == PASSES - 1),
+                )
+
+        gains = [keep.tile([P, HALF], F32, name="gain%d" % h) for h in range(HALVES)]
+        for h in range(HALVES):
+            nc.vector.tensor_copy(gains[h][:], table[:].indirect(entries(tasks, h)))
+        for h in range(HALVES):
+            result = keep.tile([N, HALF], F32, name="result%d" % h)
+            nc.vector.tensor_tensor(result[:], acc[h][:], gains[h][:], MULT)
+            nc.sync.dma_start(out=out[:, h * HALF : (h + 1) * HALF], in_=result[:])

@@ -20,6 +20,7 @@ PASSES = K // (P * PACK)
 GROUP = 16
 HALVES = 2
 HALF = S // HALVES
+QUARTER = S // 4
 QUADRANT = 32
 SCALE_ROWS = 4
 
@@ -33,7 +34,7 @@ def tile_picked_none_e_kernel(tc, xT, w1_words, w1_scales, scale, offs, task, ou
         offsets = keep.tile([P, S // GROUP], U16, name="offsets")
         tasks = keep.tile([P, S // GROUP], U16, name="tasks")
         planes = [keep.tile([P, T], F32, name="plane%d" % i) for i in range(PASSES * PACK)]
-        w_codes = keep.tile([P, PASSES, N], U32, name="w_codes", align_bytes=64)
+        w_codes = [keep.tile([P, N], U32, name="w_codes%d" % z, align_bytes=64) for z in range(PASSES)]
         w_scales = keep.tile([P, PASSES, N], U8, name="w_scales", align_bytes=64)
         table = keep.tile([P, U], F32, name="table")
 
@@ -43,11 +44,12 @@ def tile_picked_none_e_kernel(tc, xT, w1_words, w1_scales, scale, offs, task, ou
             if i == 0:
                 nc.sync.dma_start(offsets[:], offs)
         nc.sync.dma_start(tasks[:], task)
-        nc.sync.dma_start(
-            out=w_codes[:].bitcast(I32),
-            in_=w1_words.rearrange("z p c r -> p z (c r)").bitcast(I32),
-        )
         nc.sync.dma_start(out=table[:], in_=scale)
+        for z in range(PASSES):
+            nc.sync.dma_start(
+                out=w_codes[z][:].bitcast(I32),
+                in_=w1_words[z].rearrange("p c r -> p (c r)").bitcast(I32),
+            )
 
         nc.gpsimd.memset(w_scales[:].bitcast(I32), 0)
         scale_rows = w1_scales.rearrange("z (q r) c -> r q z c", r=SCALE_ROWS)
@@ -57,37 +59,88 @@ def tile_picked_none_e_kernel(tc, xT, w1_words, w1_scales, scale, offs, task, ou
                 in_=scale_rows[r].bitcast(I32),
             )
 
-        def entries(list_tile, h):
-            return list_tile[:, h * HALF // GROUP : (h + 1) * HALF // GROUP]
+        def entries(list_tile, lo, hi):
+            return list_tile[:, lo // GROUP : hi // GROUP]
 
-        acc = [psum.tile([N, HALF], F32, name="acc%d" % h) for h in range(HALVES)]
-        for z in range(PASSES):
-            grouped = [keep.tile([P, HALF, PACK], BF16, name="grouped%d_%d" % (z, h), align_bytes=64) for h in range(HALVES)]
-            for j in range(PACK):
-                for h in range(HALVES):
-                    nc.vector.tensor_copy(grouped[h][:, :, j], planes[z * PACK + j][:].indirect(entries(offsets, h)))
+        grouped = [
+            [keep.tile([P, HALF, PACK], BF16, name="grouped%d_%d" % (z, h), align_bytes=64) for h in range(HALVES)]
+            for z in range(PASSES)
+        ]
+        code_at = ((384, 512, 128, 256), (0, 128, 256, 384))
+        x_codes = keep.tile([P, S + QUARTER], U32, name="x_codes", align_bytes=64)
+        x_scales = [keep.tile([P, S], U8, name="x_scales%d" % z, align_bytes=64) for z in range(PASSES)]
+        result = keep.tile([N, S], F32, name="result")
+        pieces = ((256, 384), (384, 512), (0, 256))
+        banks = {lo: psum.tile([N, hi - lo], F32, name="acc%d" % lo) for lo, hi in pieces}
+
+        def slot(z, j, lo, hi):
+            h = lo // HALF
+            return grouped[z][h][:, lo - h * HALF : hi - h * HALF, j]
+
+        def codes(z, lo, hi):
+            at = code_at[z][lo // QUARTER]
+            return x_codes[:, at : at + hi - lo].bitcast(FP8X4)
+
+        def gather_stepped(z, j, lo, hi):
+            nc.vector.tensor_copy(slot(z, j, lo, hi), planes[z * PACK + j][:].indirect(entries(offsets, lo, hi)))
+
+        def gather_staged(z, j, lo, hi):
+            staged = keep.tile([P, hi - lo], BF16, name="staged%d_%d_%d" % (z, j, lo))
+            nc.vector.tensor_copy(staged[:], planes[z * PACK + j][:].indirect(entries(offsets, lo, hi)))
+            nc.scalar.copy(slot(z, j, lo, hi), staged[:])
+
+        def quantise(z, lo, hi):
+            h = lo // HALF
+            nc.vector.quantize_mx(
+                out=codes(z, lo, hi),
+                scales=x_scales[z][:, lo:hi],
+                in_=grouped[z][h][:, lo - h * HALF : hi - h * HALF, :].rearrange("p n j -> p (n j)"),
+            )
+
+        def product(z, lo, hi):
+            nc.tensor.matmul_mx(
+                out=banks[lo][:],
+                lhsT=w_codes[z][:].bitcast(FP8X4),
+                lhsT_scale=w_scales[:, z, :],
+                rhs=codes(z, lo, hi),
+                rhs_scale=x_scales[z][:, lo:hi],
+                start=(z == 0),
+                stop=(z == PASSES - 1),
+            )
+
+        def gain(tile, base, lo, hi):
+            nc.vector.tensor_copy(tile[:, lo - base : hi - base], table[:].indirect(entries(tasks, lo, hi)))
+
+        def finish(tile, base, lo, hi):
+            nc.vector.tensor_tensor(result[:, lo:hi], banks[lo][:], tile[:, lo - base : hi - base], MULT)
+            nc.sync.dma_start(out=out[:, lo:hi], in_=result[:, lo:hi])
+
+        for j in range(PACK):
             for h in range(HALVES):
-                x_codes = keep.tile([P, HALF], U32, name="x_codes%d_%d" % (z, h), align_bytes=64)
-                x_scales = keep.tile([P, HALF], U8, name="x_scales%d_%d" % (z, h), align_bytes=64)
-                nc.vector.quantize_mx(
-                    out=x_codes[:].bitcast(FP8X4),
-                    scales=x_scales[:],
-                    in_=grouped[h][:].rearrange("p n j -> p (n j)"),
-                )
-                nc.tensor.matmul_mx(
-                    out=acc[h][:],
-                    lhsT=w_codes[:, z, :].bitcast(FP8X4),
-                    lhsT_scale=w_scales[:, z, :],
-                    rhs=x_codes[:].bitcast(FP8X4),
-                    rhs_scale=x_scales[:],
-                    start=(z == 0),
-                    stop=(z == PASSES - 1),
-                )
-
-        gains = [keep.tile([P, HALF], F32, name="gain%d" % h) for h in range(HALVES)]
+                gather_stepped(0, j, h * HALF, (h + 1) * HALF)
         for h in range(HALVES):
-            nc.vector.tensor_copy(gains[h][:], table[:].indirect(entries(tasks, h)))
+            quantise(0, h * HALF, (h + 1) * HALF)
+        for lo, hi in pieces:
+            product(0, lo, hi)
+        for j in range(2):
+            for h in range(HALVES):
+                gather_stepped(1, j, h * HALF, (h + 1) * HALF)
         for h in range(HALVES):
-            result = keep.tile([N, HALF], F32, name="result%d" % h)
-            nc.vector.tensor_tensor(result[:], acc[h][:], gains[h][:], MULT)
-            nc.sync.dma_start(out=out[:, h * HALF : (h + 1) * HALF], in_=result[:])
+            gather_staged(1, 2, h * HALF, (h + 1) * HALF)
+        for q in range(4):
+            gather_staged(1, 3, q * QUARTER, (q + 1) * QUARTER)
+        quantise(1, 0, 128)
+        gains0 = keep.tile([P, HALF], F32, name="gains0")
+        gain(gains0, 0, 0, 256)
+        quantise(1, 128, 256)
+        product(1, 0, 256)
+        quantise(1, 256, 384)
+        product(1, 256, 384)
+        gains1 = keep.tile([P, HALF], F32, name="gains1", tag="grouped1_0", align_bytes=64)
+        gain(gains1, 256, 256, 384)
+        quantise(1, 384, 512)
+        product(1, 384, 512)
+        gain(gains1, 256, 384, 512)
+        finish(gains0, 0, 0, 256)
+        finish(gains1, 256, 256, 384)
+        finish(gains1, 256, 384, 512)

@@ -66,11 +66,11 @@ def tile_picked_none_e_kernel(tc, xT, w1_words, w1_scales, scale, offs, task, ou
             [keep.tile([P, HALF, PACK], BF16, name="grouped%d_%d" % (z, h), align_bytes=64) for h in range(HALVES)]
             for z in range(PASSES)
         ]
-        code_at = ((384, 512, 128, 256), (0, 128, 256, 384))
+        code_at = ((128, 256, 384, 512), (0, 128, 256, 384))
         x_codes = keep.tile([P, S + QUARTER], U32, name="x_codes", align_bytes=64)
         x_scales = [keep.tile([P, S], U8, name="x_scales%d" % z, align_bytes=64) for z in range(PASSES)]
         result = keep.tile([N, S], F32, name="result")
-        pieces = ((256, 384), (384, 512), (0, 256))
+        pieces = [(q * QUARTER, (q + 1) * QUARTER) for q in range(4)]
         banks = {lo: psum.tile([N, hi - lo], F32, name="acc%d" % lo) for lo, hi in pieces}
 
         def slot(z, j, lo, hi):
@@ -113,6 +113,8 @@ def tile_picked_none_e_kernel(tc, xT, w1_words, w1_scales, scale, offs, task, ou
 
         def finish(tile, base, lo, hi):
             nc.vector.tensor_tensor(result[:, lo:hi], banks[lo][:], tile[:, lo - base : hi - base], MULT)
+
+        def store(lo, hi):
             nc.sync.dma_start(out=out[:, lo:hi], in_=result[:, lo:hi])
 
         for j in range(PACK):
@@ -130,17 +132,18 @@ def tile_picked_none_e_kernel(tc, xT, w1_words, w1_scales, scale, offs, task, ou
         for q in range(4):
             gather_staged(1, 3, q * QUARTER, (q + 1) * QUARTER)
         quantise(1, 0, 128)
-        gains0 = keep.tile([P, HALF], F32, name="gains0")
-        gain(gains0, 0, 0, 256)
-        quantise(1, 128, 256)
-        product(1, 0, 256)
-        quantise(1, 256, 384)
-        product(1, 256, 384)
-        gains1 = keep.tile([P, HALF], F32, name="gains1", tag="grouped1_0", align_bytes=64)
-        gain(gains1, 256, 256, 384)
-        quantise(1, 384, 512)
-        product(1, 384, 512)
-        gain(gains1, 256, 384, 512)
-        finish(gains0, 0, 0, 256)
-        finish(gains1, 256, 256, 384)
-        finish(gains1, 256, 384, 512)
+        product(1, 0, 128)
+        gains0 = keep.tile([P, 384], F32, name="gains0")
+        gain(gains0, 0, 0, 384)
+        for lo, hi in pieces[1:]:
+            quantise(1, lo, hi)
+            product(1, lo, hi)
+        finish(gains0, 0, 0, 128)
+        store(0, 128)
+        gains1 = keep.tile([P, QUARTER], F32, name="gains1", tag="grouped1_0", align_bytes=64)
+        gain(gains1, 384, 384, 512)
+        finish(gains0, 0, 128, 256)
+        finish(gains0, 0, 256, 384)
+        store(128, 384)
+        finish(gains1, 384, 384, 512)
+        store(384, 512)

@@ -127,10 +127,10 @@ def tile_picked_none_e_kernel(tc, xT, w1_words, w1_scales, scale, offs, task, ou
         for j in range(2):
             for h in range(HALVES):
                 gather_stepped(1, j, h * HALF, (h + 1) * HALF)
-        for h in range(HALVES):
-            gather_staged(1, 2, h * HALF, (h + 1) * HALF)
-        for q in range(4):
-            gather_staged(1, 3, q * QUARTER, (q + 1) * QUARTER)
+        gather_staged(1, 2, 0, HALF)
+        gather_stepped(1, 2, HALF, S)
+        for lo, hi in ((0, 64), (64, 128), (128, 256), (256, 384), (384, 512)):
+            gather_staged(1, 3, lo, hi)
         quantise(1, 0, 128)
         product(1, 0, 128)
         gains0 = keep.tile([P, 384], F32, name="gains0")
@@ -143,7 +143,7 @@ def tile_picked_none_e_kernel(tc, xT, w1_words, w1_scales, scale, offs, task, ou
         gains1 = keep.tile([P, QUARTER], F32, name="gains1", tag="grouped1_0", align_bytes=64)
         gain(gains1, 384, 384, 512)
         finish(gains0, 0, 128, 256)
+        store(128, 256)
         finish(gains0, 0, 256, 384)
-        store(128, 384)
         finish(gains1, 384, 384, 512)
-        store(384, 512)
+        store(256, 512)

@@ -51,10 +51,10 @@ def tile_picked_none_e_kernel(tc, xT, w1_words, w1_scales, scale, offs, task, ou
                 in_=w1_words[z].rearrange("p c r -> p (c r)").bitcast(I32),
             )
 
-        nc.gpsimd.memset(w_scales[:].bitcast(I32), 0)
+        nc.vector.memset(w_scales[:].bitcast(I32), 0)
         scale_rows = w1_scales.rearrange("z (q r) c -> r q z c", r=SCALE_ROWS)
         for r in range(SCALE_ROWS):
-            nc.gpsimd.dma_start(
+            nc.scalar.dma_start(
                 out=w_scales[r:P:QUADRANT].bitcast(I32),
                 in_=scale_rows[r].bitcast(I32),
             )

@@ -13,13 +13,13 @@ U16 = mybir.dt.uint16
 U8 = mybir.dt.uint8
 FP8X4 = mybir.dt.float8_e4m3fn_x4
 MULT = mybir.AluOpType.mult
+COPY = mybir.ActivationFunctionType.Copy
 
 P = 128
 PACK = 4
 PASSES = K // (P * PACK)
 GROUP = 16
-HALVES = 2
-HALF = S // HALVES
+HALF = S // 2
 QUARTER = S // 4
 QUADRANT = 32
 SCALE_ROWS = 4
@@ -43,13 +43,13 @@ def tile_picked_none_e_kernel(tc, xT, w1_words, w1_scales, scale, offs, task, ou
             nc.sync.dma_start(out=planes[i][:], in_=rows[i // PACK, i % PACK])
             if i == 0:
                 nc.sync.dma_start(offsets[:], offs)
-        nc.sync.dma_start(tasks[:], task)
-        nc.sync.dma_start(out=table[:], in_=scale)
         for z in range(PASSES):
             nc.sync.dma_start(
                 out=w_codes[z][:].bitcast(I32),
                 in_=w1_words[z].rearrange("p c r -> p (c r)").bitcast(I32),
             )
+        nc.sync.dma_start(tasks[:], task)
+        nc.sync.dma_start(out=table[:], in_=scale)
 
         nc.vector.memset(w_scales[:].bitcast(I32), 0)
         scale_rows = w1_scales.rearrange("z (q r) c -> r q z c", r=SCALE_ROWS)
@@ -63,87 +63,80 @@ def tile_picked_none_e_kernel(tc, xT, w1_words, w1_scales, scale, offs, task, ou
             return list_tile[:, lo // GROUP : hi // GROUP]
 
         grouped = [
-            [keep.tile([P, HALF, PACK], BF16, name="grouped%d_%d" % (z, h), align_bytes=64) for h in range(HALVES)]
+            [keep.tile([P, HALF, PACK], BF16, name="grouped%d_%d" % (z, h), align_bytes=64) for h in range(2)]
             for z in range(PASSES)
         ]
-        code_at = ((128, 256, 384, 512), (0, 128, 256, 384))
-        x_codes = keep.tile([P, S + QUARTER], U32, name="x_codes", align_bytes=64)
-        x_scales = [keep.tile([P, S], U8, name="x_scales%d" % z, align_bytes=64) for z in range(PASSES)]
-        result = keep.tile([N, S], F32, name="result")
-        pieces = [(q * QUARTER, (q + 1) * QUARTER) for q in range(4)]
-        banks = {lo: psum.tile([N, hi - lo], F32, name="acc%d" % lo) for lo, hi in pieces}
+        x_codes = [keep.tile([P, S], U32, name="x_codes%d" % z, align_bytes=64) for z in range(PASSES)]
+        x_scales = {}
+        quarters = [(q * QUARTER, (q + 1) * QUARTER) for q in range(4)]
+        banks = [psum.tile([N, QUARTER], F32, name="acc%d" % q) for q in range(4)]
 
         def slot(z, j, lo, hi):
             h = lo // HALF
             return grouped[z][h][:, lo - h * HALF : hi - h * HALF, j]
 
-        def codes(z, lo, hi):
-            at = code_at[z][lo // QUARTER]
-            return x_codes[:, at : at + hi - lo].bitcast(FP8X4)
-
         def gather_stepped(z, j, lo, hi):
             nc.vector.tensor_copy(slot(z, j, lo, hi), planes[z * PACK + j][:].indirect(entries(offsets, lo, hi)))
 
         def gather_staged(z, j, lo, hi):
-            staged = keep.tile([P, hi - lo], BF16, name="staged%d_%d_%d" % (z, j, lo))
+            staged = keep.tile([P, hi - lo], BF16, name="staged%d_%d_%d" % (z, j, lo), align_bytes=64)
             nc.vector.tensor_copy(staged[:], planes[z * PACK + j][:].indirect(entries(offsets, lo, hi)))
             nc.scalar.copy(slot(z, j, lo, hi), staged[:])
 
         def quantise(z, lo, hi):
             h = lo // HALF
             nc.vector.quantize_mx(
-                out=codes(z, lo, hi),
-                scales=x_scales[z][:, lo:hi],
+                out=x_codes[z][:, lo:hi].bitcast(FP8X4),
+                scales=x_scales[z, h][:, lo - h * HALF : hi - h * HALF],
                 in_=grouped[z][h][:, lo - h * HALF : hi - h * HALF, :].rearrange("p n j -> p (n j)"),
             )
 
-        def product(z, lo, hi):
+        def product(z, q):
+            lo, hi = quarters[q]
+            h = lo // HALF
             nc.tensor.matmul_mx(
-                out=banks[lo][:],
+                out=banks[q][:],
                 lhsT=w_codes[z][:].bitcast(FP8X4),
                 lhsT_scale=w_scales[:, z, :],
-                rhs=codes(z, lo, hi),
-                rhs_scale=x_scales[z][:, lo:hi],
+                rhs=x_codes[z][:, lo:hi].bitcast(FP8X4),
+                rhs_scale=x_scales[z, h][:, lo - h * HALF : hi - h * HALF],
                 start=(z == 0),
                 stop=(z == PASSES - 1),
             )
 
-        def gain(tile, base, lo, hi):
-            nc.vector.tensor_copy(tile[:, lo - base : hi - base], table[:].indirect(entries(tasks, lo, hi)))
+        for z, h in ((0, 0), (0, 1), (1, 0)):
+            x_scales[z, h] = keep.tile([P, HALF], U8, name="x_scales%d_%d" % (z, h), align_bytes=64)
+        for i in range(PASSES * PACK - 1):
+            z, j = divmod(i, PACK)
+            gather_staged(z, j, 0, HALF)
+            gather_stepped(z, j, HALF, S)
+            if i == PACK - 1:
+                quantise(0, HALF, S)
+                quantise(0, 0, HALF)
+                for q in range(4):
+                    product(0, q)
+        gather_staged(1, 3, 0, QUARTER)
+        gather_staged(1, 3, QUARTER, HALF)
+        gather_stepped(1, 3, HALF, S)
+        x_scales[1, 1] = keep.tile([P, HALF], U8, name="x_scales1_1", tag="staged1_3_128", align_bytes=64)
+        for q in range(4):
+            quantise(1, *quarters[q])
+            product(1, q)
 
-        def finish(tile, base, lo, hi):
-            nc.vector.tensor_tensor(result[:, lo:hi], banks[lo][:], tile[:, lo - base : hi - base], MULT)
-
-        def store(lo, hi):
-            nc.sync.dma_start(out=out[:, lo:hi], in_=result[:, lo:hi])
-
-        for j in range(PACK):
-            for h in range(HALVES):
-                gather_stepped(0, j, h * HALF, (h + 1) * HALF)
-        for h in range(HALVES):
-            quantise(0, h * HALF, (h + 1) * HALF)
-        for lo, hi in pieces:
-            product(0, lo, hi)
-        for j in range(2):
-            for h in range(HALVES):
-                gather_stepped(1, j, h * HALF, (h + 1) * HALF)
-        gather_staged(1, 2, 0, HALF)
-        gather_stepped(1, 2, HALF, S)
-        for lo, hi in ((0, 64), (64, 128), (128, 256), (256, 384), (384, 512)):
-            gather_staged(1, 3, lo, hi)
-        quantise(1, 0, 128)
-        product(1, 0, 128)
-        gains0 = keep.tile([P, 384], F32, name="gains0")
-        gain(gains0, 0, 0, 384)
-        for lo, hi in pieces[1:]:
-            quantise(1, lo, hi)
-            product(1, lo, hi)
-        finish(gains0, 0, 0, 128)
-        store(0, 128)
-        gains1 = keep.tile([P, QUARTER], F32, name="gains1", tag="grouped1_0", align_bytes=64)
-        gain(gains1, 384, 384, 512)
-        finish(gains0, 0, 128, 256)
-        store(128, 256)
-        finish(gains0, 0, 256, 384)
-        finish(gains1, 384, 384, 512)
-        store(256, 512)
+        sums = [keep.tile([N, QUARTER], F32, name="sums%d" % q) for q in range(2)]
+        for q in range(2):
+            nc.scalar.copy(sums[q][:], banks[q][:])
+        gains = {q: keep.tile([P, QUARTER], F32, name="gains%d" % q) for q in (2, 3)}
+        first = keep.tile([N, QUARTER], F32, name="first")
+        upper = keep.tile([N, HALF], F32, name="upper")
+        for q in (2, 3):
+            nc.vector.tensor_copy(gains[q][:], table[:].indirect(entries(tasks, *quarters[q])))
+        nc.vector.tensor_tensor(first[:], table[:].indirect(entries(tasks, 0, QUARTER)), sums[0][:], MULT)
+        nc.sync.dma_start(out=out[:, 0:QUARTER], in_=first[:])
+        for q in (2, 3):
+            cols = slice((q - 2) * QUARTER, (q - 1) * QUARTER)
+            nc.vector.tensor_tensor(upper[:, cols], banks[q][:], gains[q][:], MULT)
+        nc.sync.dma_start(out=out[:, HALF:S], in_=upper[:])
+        second = keep.tile([N, QUARTER], F32, name="second", tag="sums0")
+        nc.vector.tensor_tensor(second[:], table[:].indirect(entries(tasks, QUARTER, HALF)), sums[1][:], MULT)
+        nc.sync.dma_start(out=out[:, QUARTER:HALF], in_=second[:])

@@ -39,10 +39,13 @@ def tile_picked_none_e_kernel(tc, xT, w1_words, w1_scales, scale, offs, task, ou
         table = keep.tile([P, U], F32, name="table")
 
         rows = xT.rearrange("(z p j) t -> z j p t", z=PASSES, j=PACK)
-        for i in range(PASSES * PACK):
+        for i in range(PASSES * PACK - 1):
             nc.sync.dma_start(out=planes[i][:], in_=rows[i // PACK, i % PACK])
             if i == 0:
                 nc.sync.dma_start(offsets[:], offs)
+        strips = ((0, 768), (768, 1280), (1280, 1792), (1792, T))
+        for lo, hi in strips:
+            nc.sync.dma_start(out=planes[-1][:, lo:hi], in_=rows[1, 3][:, lo:hi])
         for z in range(PASSES):
             nc.sync.dma_start(
                 out=w_codes[z][:].bitcast(I32),
@@ -68,8 +71,8 @@ def tile_picked_none_e_kernel(tc, xT, w1_words, w1_scales, scale, offs, task, ou
         ]
         x_codes = [keep.tile([P, S], U32, name="x_codes%d" % z, align_bytes=64) for z in range(PASSES)]
         x_scales = {}
-        quarters = [(q * QUARTER, (q + 1) * QUARTER) for q in range(4)]
-        banks = [psum.tile([N, QUARTER], F32, name="acc%d" % q) for q in range(4)]
+        pieces = [(0, QUARTER), (QUARTER, HALF), (HALF, S)]
+        banks = [psum.tile([N, hi - lo], F32, name="acc%d" % lo) for lo, hi in pieces]
 
         def slot(z, j, lo, hi):
             h = lo // HALF
@@ -92,7 +95,7 @@ def tile_picked_none_e_kernel(tc, xT, w1_words, w1_scales, scale, offs, task, ou
             )
 
         def product(z, q):
-            lo, hi = quarters[q]
+            lo, hi = pieces[q]
             h = lo // HALF
             nc.tensor.matmul_mx(
                 out=banks[q][:],
@@ -104,38 +107,41 @@ def tile_picked_none_e_kernel(tc, xT, w1_words, w1_scales, scale, offs, task, ou
                 stop=(z == PASSES - 1),
             )
 
-        for z, h in ((0, 0), (0, 1), (1, 0)):
+        for z, h in ((0, 0), (0, 1), (1, 0), (1, 1)):
             x_scales[z, h] = keep.tile([P, HALF], U8, name="x_scales%d_%d" % (z, h), align_bytes=64)
         for i in range(PASSES * PACK - 1):
             z, j = divmod(i, PACK)
-            gather_staged(z, j, 0, HALF)
+            if i < PASSES * PACK - 2:
+                gather_staged(z, j, 0, HALF)
+            else:
+                gather_stepped(z, j, 0, HALF)
             gather_stepped(z, j, HALF, S)
             if i == PACK - 1:
                 quantise(0, HALF, S)
                 quantise(0, 0, HALF)
-                for q in range(4):
+                for q in range(3):
                     product(0, q)
-        gather_staged(1, 3, 0, QUARTER)
-        gather_staged(1, 3, QUARTER, HALF)
-        gather_stepped(1, 3, HALF, S)
-        x_scales[1, 1] = keep.tile([P, HALF], U8, name="x_scales1_1", tag="staged1_3_128", align_bytes=64)
-        for q in range(4):
-            quantise(1, *quarters[q])
+        narrow = keep.tile([P, T], BF16, name="narrow")
+        for lo, hi in ((0, 768), (768, 1280), (1792, 1920)):
+            nc.scalar.copy(narrow[:, lo:hi], planes[-1][:, lo:hi])
+        for lo, hi in ((1280, 1792), (1920, T)):
+            nc.vector.tensor_copy(narrow[:, lo:hi], planes[-1][:, lo:hi])
+        gather_stepped(1, 3, 0, HALF)
+        nc.scalar.activation(slot(1, 3, HALF, S), narrow[:].indirect(entries(offsets, HALF, S)), COPY)
+        for q in range(3):
+            quantise(1, *pieces[q])
             product(1, q)
 
         sums = [keep.tile([N, QUARTER], F32, name="sums%d" % q) for q in range(2)]
         for q in range(2):
             nc.scalar.copy(sums[q][:], banks[q][:])
-        gains = {q: keep.tile([P, QUARTER], F32, name="gains%d" % q) for q in (2, 3)}
+        gains = keep.tile([P, HALF], F32, name="gains")
         first = keep.tile([N, QUARTER], F32, name="first")
         upper = keep.tile([N, HALF], F32, name="upper")
-        for q in (2, 3):
-            nc.vector.tensor_copy(gains[q][:], table[:].indirect(entries(tasks, *quarters[q])))
+        nc.vector.tensor_copy(gains[:], table[:].indirect(entries(tasks, HALF, S)))
         nc.vector.tensor_tensor(first[:], table[:].indirect(entries(tasks, 0, QUARTER)), sums[0][:], MULT)
         nc.sync.dma_start(out=out[:, 0:QUARTER], in_=first[:])
-        for q in (2, 3):
-            cols = slice((q - 2) * QUARTER, (q - 1) * QUARTER)
-            nc.vector.tensor_tensor(upper[:, cols], banks[q][:], gains[q][:], MULT)
+        nc.vector.tensor_tensor(upper[:], banks[2][:], gains[:], MULT)
         nc.sync.dma_start(out=out[:, HALF:S], in_=upper[:])
         second = keep.tile([N, QUARTER], F32, name="second", tag="sums0")
         nc.vector.tensor_tensor(second[:], table[:].indirect(entries(tasks, QUARTER, HALF)), sums[1][:], MULT)

@@ -126,7 +126,11 @@ def tile_picked_none_e_kernel(tc, xT, w1_words, w1_scales, scale, offs, task, ou
             nc.scalar.copy(narrow[:, lo:hi], planes[-1][:, lo:hi])
         for lo, hi in ((1280, 1792), (1920, T)):
             nc.vector.tensor_copy(narrow[:, lo:hi], planes[-1][:, lo:hi])
-        gather_stepped(1, 3, 0, HALF)
+        lower = [keep.tile([P, QUARTER], BF16, name="lower%d" % q) for q in range(2)]
+        for q in range(2):
+            nc.vector.tensor_copy(lower[q][:], planes[-1][:].indirect(entries(offsets, *pieces[q])))
+        for q in range(2):
+            nc.vector.tensor_copy(slot(1, 3, *pieces[q]), lower[q][:])
         nc.scalar.activation(slot(1, 3, HALF, S), narrow[:].indirect(entries(offsets, HALF, S)), COPY)
         for q in range(3):
             quantise(1, *pieces[q])

@@ -43,7 +43,7 @@ def tile_picked_none_e_kernel(tc, xT, w1_words, w1_scales, scale, offs, task, ou
             nc.sync.dma_start(out=planes[i][:], in_=rows[i // PACK, i % PACK])
             if i == 0:
                 nc.sync.dma_start(offsets[:], offs)
-        strips = ((0, 768), (768, 1280), (1280, 1792), (1792, T))
+        strips = ((0, 1024), (1024, 1792), (1792, T))
         for lo, hi in strips:
             nc.sync.dma_start(out=planes[-1][:, lo:hi], in_=rows[1, 3][:, lo:hi])
         for z in range(PASSES):
@@ -122,10 +122,9 @@ def tile_picked_none_e_kernel(tc, xT, w1_words, w1_scales, scale, offs, task, ou
                 for q in range(3):
                     product(0, q)
         narrow = keep.tile([P, T], BF16, name="narrow")
-        for lo, hi in ((0, 768), (768, 1280), (1792, 1920)):
-            nc.scalar.copy(narrow[:, lo:hi], planes[-1][:, lo:hi])
-        for lo, hi in ((1280, 1792), (1920, T)):
-            nc.vector.tensor_copy(narrow[:, lo:hi], planes[-1][:, lo:hi])
+        for (lo, hi), share in zip(strips, (768, 256, 128)):
+            nc.scalar.copy(narrow[:, lo : lo + share], planes[-1][:, lo : lo + share])
+            nc.vector.tensor_copy(narrow[:, lo + share : hi], planes[-1][:, lo + share : hi])
         lower = [keep.tile([P, QUARTER], BF16, name="lower%d" % q) for q in range(2)]
         for q in range(2):
             nc.vector.tensor_copy(lower[q][:], planes[-1][:].indirect(entries(offsets, *pieces[q])))

@@ -18,11 +18,13 @@ COPY = mybir.ActivationFunctionType.Copy
 P = 128
 PACK = 4
 PASSES = K // (P * PACK)
+PLANES = PASSES * PACK
 GROUP = 16
 HALF = S // 2
 QUARTER = S // 4
 QUADRANT = 32
 SCALE_ROWS = 4
+STRIPS = ((0, 1024, 768), (1024, 1792, 256), (1792, T, 128))
 
 
 def tile_picked_none_e_kernel(tc, xT, w1_words, w1_scales, scale, offs, task, out):
@@ -33,19 +35,18 @@ def tile_picked_none_e_kernel(tc, xT, w1_words, w1_scales, scale, offs, task, ou
 
         offsets = keep.tile([P, S // GROUP], U16, name="offsets")
         tasks = keep.tile([P, S // GROUP], U16, name="tasks")
-        planes = [keep.tile([P, T], F32, name="plane%d" % i) for i in range(PASSES * PACK)]
+        planes = [keep.tile([P, T], F32, name="plane%d" % i) for i in range(PLANES)]
         w_codes = [keep.tile([P, N], U32, name="w_codes%d" % z, align_bytes=64) for z in range(PASSES)]
         w_scales = keep.tile([P, PASSES, N], U8, name="w_scales", align_bytes=64)
         table = keep.tile([P, U], F32, name="table")
 
         rows = xT.rearrange("(z p j) t -> z j p t", z=PASSES, j=PACK)
-        for i in range(PASSES * PACK - 1):
+        for i in range(PLANES - 1):
             nc.sync.dma_start(out=planes[i][:], in_=rows[i // PACK, i % PACK])
             if i == 0:
                 nc.sync.dma_start(offsets[:], offs)
-        strips = ((0, 1024), (1024, 1792), (1792, T))
-        for lo, hi in strips:
-            nc.sync.dma_start(out=planes[-1][:, lo:hi], in_=rows[1, 3][:, lo:hi])
+        for lo, hi, share in STRIPS:
+            nc.sync.dma_start(out=planes[-1][:, lo:hi], in_=rows[PASSES - 1, PACK - 1][:, lo:hi])
         for z in range(PASSES):
             nc.sync.dma_start(
                 out=w_codes[z][:].bitcast(I32),
@@ -57,94 +58,85 @@ def tile_picked_none_e_kernel(tc, xT, w1_words, w1_scales, scale, offs, task, ou
         nc.vector.memset(w_scales[:].bitcast(I32), 0)
         scale_rows = w1_scales.rearrange("z (q r) c -> r q z c", r=SCALE_ROWS)
         for r in range(SCALE_ROWS):
-            nc.scalar.dma_start(
-                out=w_scales[r:P:QUADRANT].bitcast(I32),
-                in_=scale_rows[r].bitcast(I32),
-            )
+            nc.scalar.dma_start(out=w_scales[r:P:QUADRANT].bitcast(I32), in_=scale_rows[r].bitcast(I32))
 
         def entries(list_tile, lo, hi):
             return list_tile[:, lo // GROUP : hi // GROUP]
 
-        grouped = [
-            [keep.tile([P, HALF, PACK], BF16, name="grouped%d_%d" % (z, h), align_bytes=64) for h in range(2)]
-            for z in range(PASSES)
-        ]
+        grouped = [keep.tile([P, S * PACK], BF16, name="grouped%d" % z, align_bytes=64) for z in range(PASSES)]
         x_codes = [keep.tile([P, S], U32, name="x_codes%d" % z, align_bytes=64) for z in range(PASSES)]
-        x_scales = {}
-        pieces = [(0, QUARTER), (QUARTER, HALF), (HALF, S)]
-        banks = [psum.tile([N, hi - lo], F32, name="acc%d" % lo) for lo, hi in pieces]
 
-        def slot(z, j, lo, hi):
-            h = lo // HALF
-            return grouped[z][h][:, lo - h * HALF : hi - h * HALF, j]
+        def slot(i, lo, hi):
+            z, j = divmod(i, PACK)
+            return grouped[z][:, lo * PACK : hi * PACK].rearrange("p (n j) -> p n j", j=PACK)[:, :, j]
 
-        def gather_stepped(z, j, lo, hi):
-            nc.vector.tensor_copy(slot(z, j, lo, hi), planes[z * PACK + j][:].indirect(entries(offsets, lo, hi)))
+        def picked(i, lo, hi):
+            return planes[i][:].indirect(entries(offsets, lo, hi))
 
-        def gather_staged(z, j, lo, hi):
-            staged = keep.tile([P, hi - lo], BF16, name="staged%d_%d_%d" % (z, j, lo), align_bytes=64)
-            nc.vector.tensor_copy(staged[:], planes[z * PACK + j][:].indirect(entries(offsets, lo, hi)))
-            nc.scalar.copy(slot(z, j, lo, hi), staged[:])
+        def gather_staged(i, lo, hi):
+            staged = keep.tile([P, hi - lo], BF16, name="staged%d_%d" % (i, lo), align_bytes=64)
+            nc.vector.tensor_copy(staged[:], picked(i, lo, hi))
+            return staged
 
-        def quantise(z, lo, hi):
-            h = lo // HALF
+        def quantise(z, lo, hi, scales):
             nc.vector.quantize_mx(
-                out=x_codes[z][:, lo:hi].bitcast(FP8X4),
-                scales=x_scales[z, h][:, lo - h * HALF : hi - h * HALF],
-                in_=grouped[z][h][:, lo - h * HALF : hi - h * HALF, :].rearrange("p n j -> p (n j)"),
+                out=x_codes[z][:, lo:hi].bitcast(FP8X4), scales=scales, in_=grouped[z][:, lo * PACK : hi * PACK]
             )
 
-        def product(z, q):
-            lo, hi = pieces[q]
-            h = lo // HALF
+        def product(bank, z, lo, hi, scales, start, stop):
             nc.tensor.matmul_mx(
-                out=banks[q][:],
+                out=bank,
                 lhsT=w_codes[z][:].bitcast(FP8X4),
                 lhsT_scale=w_scales[:, z, :],
                 rhs=x_codes[z][:, lo:hi].bitcast(FP8X4),
-                rhs_scale=x_scales[z, h][:, lo - h * HALF : hi - h * HALF],
-                start=(z == 0),
-                stop=(z == PASSES - 1),
+                rhs_scale=scales,
+                start=start,
+                stop=stop,
             )
 
-        for z, h in ((0, 0), (0, 1), (1, 0), (1, 1)):
-            x_scales[z, h] = keep.tile([P, HALF], U8, name="x_scales%d_%d" % (z, h), align_bytes=64)
-        for i in range(PASSES * PACK - 1):
-            z, j = divmod(i, PACK)
-            if i < PASSES * PACK - 2:
-                gather_staged(z, j, 0, HALF)
-            else:
-                gather_stepped(z, j, 0, HALF)
-            gather_stepped(z, j, HALF, S)
+        lower_banks = [psum.tile([N, QUARTER], F32, name="lower_bank%d" % q) for q in range(2)]
+        upper_bank = psum.tile([N, HALF], F32, name="upper_bank")
+
+        first_scales = keep.tile([P, S], U8, name="first_scales", align_bytes=64)
+        for i in range(PLANES - 1):
+            placed = HALF if i < PLANES - 2 else S - QUARTER
+            staged = gather_staged(i, placed, S)
+            nc.scalar.copy(slot(i, placed, S), staged[:])
+            nc.vector.tensor_copy(slot(i, 0, placed), picked(i, 0, placed))
             if i == PACK - 1:
-                quantise(0, HALF, S)
-                quantise(0, 0, HALF)
-                for q in range(3):
-                    product(0, q)
-        narrow = keep.tile([P, T], BF16, name="narrow")
-        for (lo, hi), share in zip(strips, (768, 256, 128)):
-            nc.scalar.copy(narrow[:, lo : lo + share], planes[-1][:, lo : lo + share])
-            nc.vector.tensor_copy(narrow[:, lo + share : hi], planes[-1][:, lo + share : hi])
-        lower = [keep.tile([P, QUARTER], BF16, name="lower%d" % q) for q in range(2)]
+                for lo in (0, HALF):
+                    quantise(0, lo, lo + HALF, first_scales[:, lo : lo + HALF])
+                for q in range(2):
+                    lo = q * QUARTER
+                    product(lower_banks[q][:], 0, lo, lo + QUARTER, first_scales[:, lo : lo + QUARTER], True, False)
+                product(upper_bank[:], 0, HALF, S, first_scales[:, HALF:S], True, False)
+
+        last = PLANES - 1
+        narrow = keep.tile([P, T], BF16, name="narrow", align_bytes=64)
+        for lo, hi, share in STRIPS:
+            nc.scalar.copy(narrow[:, lo : lo + share], planes[last][:, lo : lo + share])
+            nc.vector.tensor_copy(narrow[:, lo + share : hi], planes[last][:, lo + share : hi])
+        lower = [gather_staged(last, q * QUARTER, (q + 1) * QUARTER) for q in range(2)]
         for q in range(2):
-            nc.vector.tensor_copy(lower[q][:], planes[-1][:].indirect(entries(offsets, *pieces[q])))
-        for q in range(2):
-            nc.vector.tensor_copy(slot(1, 3, *pieces[q]), lower[q][:])
-        nc.scalar.activation(slot(1, 3, HALF, S), narrow[:].indirect(entries(offsets, HALF, S)), COPY)
-        for q in range(3):
-            quantise(1, *pieces[q])
-            product(1, q)
+            nc.vector.tensor_copy(slot(last, q * QUARTER, (q + 1) * QUARTER), lower[q][:])
+        nc.scalar.activation(slot(last, HALF, S), narrow[:].indirect(entries(offsets, HALF, S)), COPY)
+
+        pieces = ((0, QUARTER, lower_banks[0]), (QUARTER, HALF, lower_banks[1]), (HALF, S, upper_bank))
+        for lo, hi, bank in pieces:
+            scales = keep.tile([P, hi - lo], U8, name="last_scales%d" % lo, align_bytes=64)
+            quantise(1, lo, hi, scales[:])
+            product(bank[:], 1, lo, hi, scales[:], False, True)
 
         sums = [keep.tile([N, QUARTER], F32, name="sums%d" % q) for q in range(2)]
         for q in range(2):
-            nc.scalar.copy(sums[q][:], banks[q][:])
+            nc.scalar.copy(sums[q][:], lower_banks[q][:])
         gains = keep.tile([P, HALF], F32, name="gains")
         first = keep.tile([N, QUARTER], F32, name="first")
         upper = keep.tile([N, HALF], F32, name="upper")
         nc.vector.tensor_copy(gains[:], table[:].indirect(entries(tasks, HALF, S)))
         nc.vector.tensor_tensor(first[:], table[:].indirect(entries(tasks, 0, QUARTER)), sums[0][:], MULT)
         nc.sync.dma_start(out=out[:, 0:QUARTER], in_=first[:])
-        nc.vector.tensor_tensor(upper[:], banks[2][:], gains[:], MULT)
+        nc.vector.tensor_tensor(upper[:], upper_bank[:], gains[:], MULT)
         nc.sync.dma_start(out=out[:, HALF:S], in_=upper[:])
         second = keep.tile([N, QUARTER], F32, name="second", tag="sums0")
         nc.vector.tensor_tensor(second[:], table[:].indirect(entries(tasks, QUARTER, HALF)), sums[1][:], MULT)

@@ -24,7 +24,7 @@ HALF = S // 2
 QUARTER = S // 4
 QUADRANT = 32
 SCALE_ROWS = 4
-STRIPS = ((0, 1024, 768), (1024, 1792, 256), (1792, T, 128))
+STRIPS = ((0, 1408, 512), (1408, 1920, 128), (1920, T, 128))
 
 
 def tile_picked_none_e_kernel(tc, xT, w1_words, w1_scales, scale, offs, task, out):
@@ -55,7 +55,6 @@ def tile_picked_none_e_kernel(tc, xT, w1_words, w1_scales, scale, offs, task, ou
         nc.sync.dma_start(tasks[:], task)
         nc.sync.dma_start(out=table[:], in_=scale)
 
-        nc.vector.memset(w_scales[:].bitcast(I32), 0)
         scale_rows = w1_scales.rearrange("z (q r) c -> r q z c", r=SCALE_ROWS)
         for r in range(SCALE_ROWS):
             nc.scalar.dma_start(out=w_scales[r:P:QUADRANT].bitcast(I32), in_=scale_rows[r].bitcast(I32))
@@ -99,10 +98,11 @@ def tile_picked_none_e_kernel(tc, xT, w1_words, w1_scales, scale, offs, task, ou
 
         first_scales = keep.tile([P, S], U8, name="first_scales", align_bytes=64)
         for i in range(PLANES - 1):
-            placed = HALF if i < PLANES - 2 else S - QUARTER
-            staged = gather_staged(i, placed, S)
-            nc.scalar.copy(slot(i, placed, S), staged[:])
-            nc.vector.tensor_copy(slot(i, 0, placed), picked(i, 0, placed))
+            width = HALF if i < PLANES - 2 else QUARTER
+            for lo in range(HALF, S, width):
+                staged = gather_staged(i, lo, lo + width)
+                nc.scalar.copy(slot(i, lo, lo + width), staged[:])
+            nc.vector.tensor_copy(slot(i, 0, HALF), picked(i, 0, HALF))
             if i == PACK - 1:
                 for lo in (0, HALF):
                     quantise(0, lo, lo + HALF, first_scales[:, lo : lo + HALF])
@@ -114,8 +114,10 @@ def tile_picked_none_e_kernel(tc, xT, w1_words, w1_scales, scale, offs, task, ou
         last = PLANES - 1
         narrow = keep.tile([P, T], BF16, name="narrow", align_bytes=64)
         for lo, hi, share in STRIPS:
-            nc.scalar.copy(narrow[:, lo : lo + share], planes[last][:, lo : lo + share])
-            nc.vector.tensor_copy(narrow[:, lo + share : hi], planes[last][:, lo + share : hi])
+            if share > 0:
+                nc.scalar.copy(narrow[:, lo : lo + share], planes[last][:, lo : lo + share])
+            if lo + share < hi:
+                nc.vector.tensor_copy(narrow[:, lo + share : hi], planes[last][:, lo + share : hi])
         lower = [gather_staged(last, q * QUARTER, (q + 1) * QUARTER) for q in range(2)]
         for q in range(2):
             nc.vector.tensor_copy(slot(last, q * QUARTER, (q + 1) * QUARTER), lower[q][:])

@@ -96,13 +96,18 @@ def tile_picked_none_e_kernel(tc, xT, w1_words, w1_scales, scale, offs, task, ou
         lower_banks = [psum.tile([N, QUARTER], F32, name="lower_bank%d" % q) for q in range(2)]
         upper_bank = psum.tile([N, HALF], F32, name="upper_bank")
 
+        pairs = [keep.tile([P, 2, QUARTER], BF16, name="pair%d" % q, align_bytes=64) for q in range(2)]
         first_scales = keep.tile([P, S], U8, name="first_scales", align_bytes=64)
         for i in range(PLANES - 1):
             width = HALF if i < PLANES - 2 else QUARTER
             for lo in range(HALF, S, width):
                 staged = gather_staged(i, lo, lo + width)
                 nc.scalar.copy(slot(i, lo, lo + width), staged[:])
-            nc.vector.tensor_copy(slot(i, 0, HALF), picked(i, 0, HALF))
+            if i < PLANES - 2:
+                nc.vector.tensor_copy(slot(i, 0, HALF), picked(i, 0, HALF))
+            else:
+                for q in range(2):
+                    nc.vector.tensor_copy(pairs[q][:, 0, :], picked(i, q * QUARTER, (q + 1) * QUARTER))
             if i == PACK - 1:
                 for lo in (0, HALF):
                     quantise(0, lo, lo + HALF, first_scales[:, lo : lo + HALF])
@@ -118,9 +123,11 @@ def tile_picked_none_e_kernel(tc, xT, w1_words, w1_scales, scale, offs, task, ou
                 nc.scalar.copy(narrow[:, lo : lo + share], planes[last][:, lo : lo + share])
             if lo + share < hi:
                 nc.vector.tensor_copy(narrow[:, lo + share : hi], planes[last][:, lo + share : hi])
-        lower = [gather_staged(last, q * QUARTER, (q + 1) * QUARTER) for q in range(2)]
         for q in range(2):
-            nc.vector.tensor_copy(slot(last, q * QUARTER, (q + 1) * QUARTER), lower[q][:])
+            nc.vector.tensor_copy(pairs[q][:, 1, :], picked(last, q * QUARTER, (q + 1) * QUARTER))
+        for q in range(2):
+            tokens = grouped[1][:, q * QUARTER * PACK : (q + 1) * QUARTER * PACK].rearrange("p (n j) -> p n j", j=PACK)
+            nc.vector.tensor_copy(tokens[:, :, 2:4], pairs[q][:].rearrange("p j n -> p n j"))
         nc.scalar.activation(slot(last, HALF, S), narrow[:].indirect(entries(offsets, HALF, S)), COPY)
 
         pieces = ((0, QUARTER, lower_banks[0]), (QUARTER, HALF, lower_banks[1]), (HALF, S, upper_bank))

@@ -24,7 +24,7 @@ HALF = S // 2
 QUARTER = S // 4
 QUADRANT = 32
 SCALE_ROWS = 4
-STRIPS = ((0, 1408, 512), (1408, 1920, 128), (1920, T, 128))
+STRIPS = ((0, 1216, 448), (1216, 1728, 128), (1728, 1984, 0), (1984, T, 64))
 
 
 def tile_picked_none_e_kernel(tc, xT, w1_words, w1_scales, scale, offs, task, out):
@@ -35,16 +35,17 @@ def tile_picked_none_e_kernel(tc, xT, w1_words, w1_scales, scale, offs, task, ou
 
         offsets = keep.tile([P, S // GROUP], U16, name="offsets")
         tasks = keep.tile([P, S // GROUP], U16, name="tasks")
-        planes = [keep.tile([P, T], F32, name="plane%d" % i) for i in range(PLANES)]
+        head = keep.tile([P, 2 * T], F32, name="head")
+        planes = [head, head[:, T : 2 * T]] + [keep.tile([P, T], F32, name="plane%d" % i) for i in range(2, PLANES)]
         w_codes = [keep.tile([P, N], U32, name="w_codes%d" % z, align_bytes=64) for z in range(PASSES)]
         w_scales = keep.tile([P, PASSES, N], U8, name="w_scales", align_bytes=64)
         table = keep.tile([P, U], F32, name="table")
 
         rows = xT.rearrange("(z p j) t -> z j p t", z=PASSES, j=PACK)
-        for i in range(PLANES - 1):
+        nc.sync.dma_start(out=head[:], in_=xT.rearrange("(z p h j) t -> z h p (j t)", z=PASSES, h=2, j=2)[0, 0])
+        nc.sync.dma_start(offsets[:], offs)
+        for i in range(2, PLANES - 1):
             nc.sync.dma_start(out=planes[i][:], in_=rows[i // PACK, i % PACK])
-            if i == 0:
-                nc.sync.dma_start(offsets[:], offs)
         for lo, hi, share in STRIPS:
             nc.sync.dma_start(out=planes[-1][:, lo:hi], in_=rows[PASSES - 1, PACK - 1][:, lo:hi])
         for z in range(PASSES):
@@ -69,11 +70,12 @@ def tile_picked_none_e_kernel(tc, xT, w1_words, w1_scales, scale, offs, task, ou
             z, j = divmod(i, PACK)
             return grouped[z][:, lo * PACK : hi * PACK].rearrange("p (n j) -> p n j", j=PACK)[:, :, j]
 
-        def picked(i, lo, hi):
-            return planes[i][:].indirect(entries(offsets, lo, hi))
+        def picked(i, lo, hi, part=False):
+            window = head[:, 0:T] if part else planes[i][:]
+            return window.indirect(entries(offsets, lo, hi))
 
         def gather_staged(i, lo, hi):
-            staged = keep.tile([P, hi - lo], BF16, name="staged%d_%d" % (i, lo), align_bytes=64)
+            staged = keep.tile([P, hi - lo], F32 if i == 1 else BF16, name="staged%d_%d" % (i, lo), align_bytes=64)
             nc.vector.tensor_copy(staged[:], picked(i, lo, hi))
             return staged
 
@@ -104,7 +106,7 @@ def tile_picked_none_e_kernel(tc, xT, w1_words, w1_scales, scale, offs, task, ou
                 staged = gather_staged(i, lo, lo + width)
                 nc.scalar.copy(slot(i, lo, lo + width), staged[:])
             if i < PLANES - 2:
-                nc.vector.tensor_copy(slot(i, 0, HALF), picked(i, 0, HALF))
+                nc.vector.tensor_copy(slot(i, 0, HALF), picked(i, 0, HALF, i == 0))
             else:
                 for q in range(2):
                     nc.vector.tensor_copy(pairs[q][:, 0, :], picked(i, q * QUARTER, (q + 1) * QUARTER))

@@ -24,7 +24,7 @@ HALF = S // 2
 QUARTER = S // 4
 QUADRANT = 32
 SCALE_ROWS = 4
-STRIPS = ((0, 1216, 448), (1216, 1728, 128), (1728, 1984, 0), (1984, T, 64))
+STRIPS = ((0, 1216, 512), (1216, 1728, 192), (1728, 1984, 0), (1984, T, 64))
 
 
 def tile_picked_none_e_kernel(tc, xT, w1_words, w1_scales, scale, offs, task, out):
@@ -98,7 +98,7 @@ def tile_picked_none_e_kernel(tc, xT, w1_words, w1_scales, scale, offs, task, ou
         lower_banks = [psum.tile([N, QUARTER], F32, name="lower_bank%d" % q) for q in range(2)]
         upper_bank = psum.tile([N, HALF], F32, name="upper_bank")
 
-        pairs = [keep.tile([P, 2, QUARTER], BF16, name="pair%d" % q, align_bytes=64) for q in range(2)]
+        pair = keep.tile([P, 2, QUARTER], BF16, name="pair", align_bytes=64)
         first_scales = keep.tile([P, S], U8, name="first_scales", align_bytes=64)
         for i in range(PLANES - 1):
             width = HALF if i < PLANES - 2 else QUARTER
@@ -108,8 +108,9 @@ def tile_picked_none_e_kernel(tc, xT, w1_words, w1_scales, scale, offs, task, ou
             if i < PLANES - 2:
                 nc.vector.tensor_copy(slot(i, 0, HALF), picked(i, 0, HALF, i == 0))
             else:
-                for q in range(2):
-                    nc.vector.tensor_copy(pairs[q][:, 0, :], picked(i, q * QUARTER, (q + 1) * QUARTER))
+                staged = gather_staged(i, 0, QUARTER)
+                nc.vector.tensor_copy(pair[:, 0, :], picked(i, QUARTER, HALF))
+                nc.vector.tensor_copy(slot(i, 0, QUARTER), staged[:])
             if i == PACK - 1:
                 for lo in (0, HALF):
                     quantise(0, lo, lo + HALF, first_scales[:, lo : lo + HALF])
@@ -125,11 +126,11 @@ def tile_picked_none_e_kernel(tc, xT, w1_words, w1_scales, scale, offs, task, ou
                 nc.scalar.copy(narrow[:, lo : lo + share], planes[last][:, lo : lo + share])
             if lo + share < hi:
                 nc.vector.tensor_copy(narrow[:, lo + share : hi], planes[last][:, lo + share : hi])
-        for q in range(2):
-            nc.vector.tensor_copy(pairs[q][:, 1, :], picked(last, q * QUARTER, (q + 1) * QUARTER))
-        for q in range(2):
-            tokens = grouped[1][:, q * QUARTER * PACK : (q + 1) * QUARTER * PACK].rearrange("p (n j) -> p n j", j=PACK)
-            nc.vector.tensor_copy(tokens[:, :, 2:4], pairs[q][:].rearrange("p j n -> p n j"))
+        staged = gather_staged(last, 0, QUARTER)
+        nc.vector.tensor_copy(pair[:, 1, :], picked(last, QUARTER, HALF))
+        nc.vector.tensor_copy(slot(last, 0, QUARTER), staged[:])
+        tokens = grouped[1][:, QUARTER * PACK : HALF * PACK].rearrange("p (n j) -> p n j", j=PACK)
+        nc.vector.tensor_copy(tokens[:, :, 2:4], pair[:].rearrange("p j n -> p n j"))
         nc.scalar.activation(slot(last, HALF, S), narrow[:].indirect(entries(offsets, HALF, S)), COPY)
 
         pieces = ((0, QUARTER, lower_banks[0]), (QUARTER, HALF, lower_banks[1]), (HALF, S, upper_bank))

@@ -24,7 +24,7 @@ HALF = S // 2
 QUARTER = S // 4
 QUADRANT = 32
 SCALE_ROWS = 4
-STRIPS = ((0, 1216, 512), (1216, 1728, 192), (1728, 1984, 0), (1984, T, 64))
+STRIPS = ((0, 1216, 512), (1216, 1728, 192), (1728, 1984, 128), (1984, T, 0))
 
 
 def tile_picked_none_e_kernel(tc, xT, w1_words, w1_scales, scale, offs, task, out):

@@ -95,8 +95,7 @@ def tile_picked_none_e_kernel(tc, xT, w1_words, w1_scales, scale, offs, task, ou
                 stop=stop,
             )
 
-        lower_banks = [psum.tile([N, QUARTER], F32, name="lower_bank%d" % q) for q in range(2)]
-        upper_bank = psum.tile([N, HALF], F32, name="upper_bank")
+        banks = [psum.tile([N, QUARTER], F32, name="bank%d" % q) for q in range(4)]
 
         pair = keep.tile([P, 2, QUARTER], BF16, name="pair", align_bytes=64)
         first_scales = keep.tile([P, S], U8, name="first_scales", align_bytes=64)
@@ -114,10 +113,9 @@ def tile_picked_none_e_kernel(tc, xT, w1_words, w1_scales, scale, offs, task, ou
             if i == PACK - 1:
                 for lo in (0, HALF):
                     quantise(0, lo, lo + HALF, first_scales[:, lo : lo + HALF])
-                for q in range(2):
+                for q in range(4):
                     lo = q * QUARTER
-                    product(lower_banks[q][:], 0, lo, lo + QUARTER, first_scales[:, lo : lo + QUARTER], True, False)
-                product(upper_bank[:], 0, HALF, S, first_scales[:, HALF:S], True, False)
+                    product(banks[q][:], 0, lo, lo + QUARTER, first_scales[:, lo : lo + QUARTER], True, False)
 
         last = PLANES - 1
         narrow = keep.tile([P, T], BF16, name="narrow", align_bytes=64)
@@ -133,22 +131,24 @@ def tile_picked_none_e_kernel(tc, xT, w1_words, w1_scales, scale, offs, task, ou
         nc.vector.tensor_copy(tokens[:, :, 2:4], pair[:].rearrange("p j n -> p n j"))
         nc.scalar.activation(slot(last, HALF, S), narrow[:].indirect(entries(offsets, HALF, S)), COPY)
 
-        pieces = ((0, QUARTER, lower_banks[0]), (QUARTER, HALF, lower_banks[1]), (HALF, S, upper_bank))
-        for lo, hi, bank in pieces:
+        for q, bank in enumerate(banks):
+            lo, hi = q * QUARTER, (q + 1) * QUARTER
             scales = keep.tile([P, hi - lo], U8, name="last_scales%d" % lo, align_bytes=64)
             quantise(1, lo, hi, scales[:])
             product(bank[:], 1, lo, hi, scales[:], False, True)
 
         sums = [keep.tile([N, QUARTER], F32, name="sums%d" % q) for q in range(2)]
         for q in range(2):
-            nc.scalar.copy(sums[q][:], lower_banks[q][:])
+            nc.scalar.copy(sums[q][:], banks[q][:])
         gains = keep.tile([P, HALF], F32, name="gains")
         first = keep.tile([N, QUARTER], F32, name="first")
         upper = keep.tile([N, HALF], F32, name="upper")
         nc.vector.tensor_copy(gains[:], table[:].indirect(entries(tasks, HALF, S)))
         nc.vector.tensor_tensor(first[:], table[:].indirect(entries(tasks, 0, QUARTER)), sums[0][:], MULT)
         nc.sync.dma_start(out=out[:, 0:QUARTER], in_=first[:])
-        nc.vector.tensor_tensor(upper[:], upper_bank[:], gains[:], MULT)
+        for q in range(2):
+            cols = slice(q * QUARTER, (q + 1) * QUARTER)
+            nc.vector.tensor_tensor(upper[:, cols], banks[2 + q][:], gains[:, cols], MULT)
         nc.sync.dma_start(out=out[:, HALF:S], in_=upper[:])
         second = keep.tile([N, QUARTER], F32, name="second", tag="sums0")
         nc.vector.tensor_tensor(second[:], table[:].indirect(entries(tasks, QUARTER, HALF)), sums[1][:], MULT)

@@ -24,6 +24,8 @@ HALF = S // 2
 QUARTER = S // 4
 QUADRANT = 32
 SCALE_ROWS = 4
+VECTOR_GAINS = (160, 320)
+SCALAR_GAINS = ((0, 160), (384, 512), (320, 384))
 STRIPS = ((0, 1216, 512), (1216, 1728, 192), (1728, 1984, 128), (1984, T, 0))
 
 
@@ -137,19 +139,15 @@ def tile_picked_none_e_kernel(tc, xT, w1_words, w1_scales, scale, offs, task, ou
             quantise(1, lo, hi, scales[:])
             product(bank[:], 1, lo, hi, scales[:], False, True)
 
-        sums = [keep.tile([N, QUARTER], F32, name="sums%d" % q) for q in range(2)]
-        for q in range(2):
-            nc.scalar.copy(sums[q][:], banks[q][:])
-        gains = keep.tile([P, HALF], F32, name="gains")
-        first = keep.tile([N, QUARTER], F32, name="first")
-        upper = keep.tile([N, HALF], F32, name="upper")
-        nc.vector.tensor_copy(gains[:], table[:].indirect(entries(tasks, HALF, S)))
-        nc.vector.tensor_tensor(first[:], table[:].indirect(entries(tasks, 0, QUARTER)), sums[0][:], MULT)
-        nc.sync.dma_start(out=out[:, 0:QUARTER], in_=first[:])
-        for q in range(2):
-            cols = slice(q * QUARTER, (q + 1) * QUARTER)
-            nc.vector.tensor_tensor(upper[:, cols], banks[2 + q][:], gains[:, cols], MULT)
-        nc.sync.dma_start(out=out[:, HALF:S], in_=upper[:])
-        second = keep.tile([N, QUARTER], F32, name="second", tag="sums0")
-        nc.vector.tensor_tensor(second[:], table[:].indirect(entries(tasks, QUARTER, HALF)), sums[1][:], MULT)
-        nc.sync.dma_start(out=out[:, QUARTER:HALF], in_=second[:])
+        gains = keep.tile([P, S], F32, name="gains")
+        result = keep.tile([N, S], F32, name="result")
+        for lo, hi in SCALAR_GAINS:
+            nc.scalar.activation(gains[:, lo:hi], table[:].indirect(entries(tasks, lo, hi)), COPY)
+        lo, hi = VECTOR_GAINS
+        nc.vector.tensor_copy(gains[:, lo:hi], table[:].indirect(entries(tasks, lo, hi)))
+        for group in ((0, 1), (3,), (2,)):
+            for q in group:
+                cols = slice(q * QUARTER, (q + 1) * QUARTER)
+                nc.vector.tensor_tensor(result[:, cols], banks[q][:], gains[:, cols], MULT)
+            cols = slice(group[0] * QUARTER, (group[-1] + 1) * QUARTER)
+            nc.sync.dma_start(out=out[:, cols], in_=result[:, cols])

@@ -26,6 +26,9 @@ QUADRANT = 32
 SCALE_ROWS = 4
 VECTOR_GAINS = (160, 320)
 SCALAR_GAINS = ((0, 160), (384, 512), (320, 384))
+STRETCH = 32 * 1024
+PLANE_BYTES = 4 * T
+PLANE_AT = {2: STRETCH, 3: 2 * STRETCH + PLANE_BYTES, 4: 2 * PLANE_BYTES, 5: STRETCH + PLANE_BYTES, 6: 2 * STRETCH + 2 * PLANE_BYTES, 7: 3 * PLANE_BYTES}
 STRIPS = ((0, 1216, 512), (1216, 1728, 192), (1728, 1984, 128), (1984, T, 0))
 
 
@@ -35,13 +38,13 @@ def tile_picked_none_e_kernel(tc, xT, w1_words, w1_scales, scale, offs, task, ou
         keep = ctx.enter_context(tc.tile_pool(name="keep", bufs=1))
         psum = ctx.enter_context(tc.psum_pool(name="psum", bufs=1))
 
-        offsets = keep.tile([P, S // GROUP], U16, name="offsets")
-        tasks = keep.tile([P, S // GROUP], U16, name="tasks")
-        head = keep.tile([P, 2 * T], F32, name="head")
-        planes = [head, head[:, T : 2 * T]] + [keep.tile([P, T], F32, name="plane%d" % i) for i in range(2, PLANES)]
-        w_codes = [keep.tile([P, N], U32, name="w_codes%d" % z, align_bytes=64) for z in range(PASSES)]
-        w_scales = keep.tile([P, PASSES, N], U8, name="w_scales", align_bytes=64)
-        table = keep.tile([P, U], F32, name="table")
+        offsets = keep.tile([P, S // GROUP], U16, name="offsets", offset=5 * STRETCH + 8192)
+        tasks = keep.tile([P, S // GROUP], U16, name="tasks", offset=5 * STRETCH + 8256)
+        head = keep.tile([P, 2 * T], F32, name="head", offset=0, align_bytes=STRETCH)
+        planes = [head, head[:, T : 2 * T]] + [keep.tile([P, T], F32, name="plane%d" % i, offset=PLANE_AT[i]) for i in range(2, PLANES)]
+        w_codes = [keep.tile([P, N], U32, name="w_codes%d" % z, align_bytes=64, offset=STRETCH + 2 * PLANE_BYTES + 512 * z) for z in range(PASSES)]
+        w_scales = keep.tile([P, PASSES, N], U8, name="w_scales", align_bytes=64, offset=STRETCH + 2 * PLANE_BYTES + 1024)
+        table = keep.tile([P, U], F32, name="table", offset=2 * STRETCH - 2 * U)
 
         rows = xT.rearrange("(z p j) t -> z j p t", z=PASSES, j=PACK)
         nc.sync.dma_start(out=head[:], in_=xT.rearrange("(z p h j) t -> z h p (j t)", z=PASSES, h=2, j=2)[0, 0])
@@ -65,8 +68,8 @@ def tile_picked_none_e_kernel(tc, xT, w1_words, w1_scales, scale, offs, task, ou
         def entries(list_tile, lo, hi):
             return list_tile[:, lo // GROUP : hi // GROUP]
 
-        grouped = [keep.tile([P, S * PACK], BF16, name="grouped%d" % z, align_bytes=64) for z in range(PASSES)]
-        x_codes = [keep.tile([P, S], U32, name="x_codes%d" % z, align_bytes=64) for z in range(PASSES)]
+        grouped = [keep.tile([P, S * PACK], BF16, name="grouped%d" % z, align_bytes=64, offset=(3 + 2 * z) * STRETCH - S * PACK) for z in range(PASSES)]
+        x_codes = [keep.tile([P, S], U32, name="x_codes%d" % z, align_bytes=64, offset=4 * STRETCH + 16384 + 2048 * z) for z in range(PASSES)]
 
         def slot(i, lo, hi):
             z, j = divmod(i, PACK)
@@ -77,7 +80,7 @@ def tile_picked_none_e_kernel(tc, xT, w1_words, w1_scales, scale, offs, task, ou
             return window.indirect(entries(offsets, lo, hi))
 
         def gather_staged(i, lo, hi):
-            staged = keep.tile([P, hi - lo], F32 if i == 1 else BF16, name="staged%d_%d" % (i, lo), align_bytes=64)
+            staged = keep.tile([P, hi - lo], F32 if i == 1 else BF16, name="staged%d_%d" % (i, lo), align_bytes=64, offset=4 * STRETCH + 2048 * i + 2 * lo)
             nc.vector.tensor_copy(staged[:], picked(i, lo, hi))
             return staged
 
@@ -99,8 +102,8 @@ def tile_picked_none_e_kernel(tc, xT, w1_words, w1_scales, scale, offs, task, ou
 
         banks = [psum.tile([N, QUARTER], F32, name="bank%d" % q) for q in range(4)]
 
-        pair = keep.tile([P, 2, QUARTER], BF16, name="pair", align_bytes=64)
-        first_scales = keep.tile([P, S], U8, name="first_scales", align_bytes=64)
+        pair = keep.tile([P, 2, QUARTER], BF16, name="pair", align_bytes=64, offset=4 * STRETCH + 20480)
+        first_scales = keep.tile([P, S], U8, name="first_scales", align_bytes=64, offset=4 * STRETCH + 21504)
         for i in range(PLANES - 1):
             width = HALF if i < PLANES - 2 else QUARTER
             for lo in range(HALF, S, width):
@@ -120,7 +123,7 @@ def tile_picked_none_e_kernel(tc, xT, w1_words, w1_scales, scale, offs, task, ou
                     product(banks[q][:], 0, lo, lo + QUARTER, first_scales[:, lo : lo + QUARTER], True, False)
 
         last = PLANES - 1
-        narrow = keep.tile([P, T], BF16, name="narrow", align_bytes=64)
+        narrow = keep.tile([P, T], BF16, name="narrow", align_bytes=64, offset=3 * STRETCH + 8192)
         for lo, hi, share in STRIPS:
             if share > 0:
                 nc.scalar.copy(narrow[:, lo : lo + share], planes[last][:, lo : lo + share])
@@ -135,12 +138,12 @@ def tile_picked_none_e_kernel(tc, xT, w1_words, w1_scales, scale, offs, task, ou
 
         for q, bank in enumerate(banks):
             lo, hi = q * QUARTER, (q + 1) * QUARTER
-            scales = keep.tile([P, hi - lo], U8, name="last_scales%d" % lo, align_bytes=64)
+            scales = keep.tile([P, hi - lo], U8, name="last_scales%d" % lo, align_bytes=64, offset=4 * STRETCH + 22528 + lo)
             quantise(1, lo, hi, scales[:])
             product(bank[:], 1, lo, hi, scales[:], False, True)
 
-        gains = keep.tile([P, S], F32, name="gains")
-        result = keep.tile([N, S], F32, name="result")
+        gains = keep.tile([P, S], F32, name="gains", offset=3 * STRETCH + 16384)
+        result = keep.tile([N, S], F32, name="result", offset=4 * STRETCH + 24576)
         for lo, hi in SCALAR_GAINS:
             nc.scalar.activation(gains[:, lo:hi], table[:].indirect(entries(tasks, lo, hi)), COPY)
         lo, hi = VECTOR_GAINS

from contextlib import ExitStack

import concourse.mybir as mybir

K, T, S, N, U = 1024, 2048, 512, 128, 1024
FLOPS = 2 * K * S * N

F32 = mybir.dt.float32
BF16 = mybir.dt.bfloat16
I32 = mybir.dt.int32
U32 = mybir.dt.uint32
U16 = mybir.dt.uint16
U8 = mybir.dt.uint8
FP8X4 = mybir.dt.float8_e4m3fn_x4
MULT = mybir.AluOpType.mult
COPY = mybir.ActivationFunctionType.Copy

P = 128
PACK = 4
PASSES = K // (P * PACK)
PLANES = PASSES * PACK
GROUP = 16
HALF = S // 2
QUARTER = S // 4
QUADRANT = 32
SCALE_ROWS = 4
VECTOR_GAINS = (160, 320)
SCALAR_GAINS = ((0, 160), (384, 512), (320, 384))
STRETCH = 32 * 1024
PLANE_BYTES = 4 * T
PLANE_AT = {2: STRETCH, 3: 2 * STRETCH + PLANE_BYTES, 4: 2 * PLANE_BYTES, 5: STRETCH + PLANE_BYTES, 6: 2 * STRETCH + 2 * PLANE_BYTES, 7: 3 * PLANE_BYTES}
STRIPS = ((0, 1216, 512), (1216, 1728, 192), (1728, 1984, 128), (1984, T, 0))


def tile_picked_none_e_kernel(tc, xT, w1_words, w1_scales, scale, offs, task, out):
    nc = tc.nc
    with ExitStack() as ctx:
        keep = ctx.enter_context(tc.tile_pool(name="keep", bufs=1))
        psum = ctx.enter_context(tc.psum_pool(name="psum", bufs=1))

        offsets = keep.tile([P, S // GROUP], U16, name="offsets", offset=5 * STRETCH + 8192)
        tasks = keep.tile([P, S // GROUP], U16, name="tasks", offset=5 * STRETCH + 8256)
        head = keep.tile([P, 2 * T], F32, name="head", offset=0, align_bytes=STRETCH)
        planes = [head, head[:, T : 2 * T]] + [keep.tile([P, T], F32, name="plane%d" % i, offset=PLANE_AT[i]) for i in range(2, PLANES)]
        w_codes = [keep.tile([P, N], U32, name="w_codes%d" % z, align_bytes=64, offset=STRETCH + 2 * PLANE_BYTES + 512 * z) for z in range(PASSES)]
        w_scales = keep.tile([P, PASSES, N], U8, name="w_scales", align_bytes=64, offset=STRETCH + 2 * PLANE_BYTES + 1024)
        table = keep.tile([P, U], F32, name="table", offset=2 * STRETCH - 2 * U)

        rows = xT.rearrange("(z p j) t -> z j p t", z=PASSES, j=PACK)
        nc.sync.dma_start(out=head[:], in_=xT.rearrange("(z p h j) t -> z h p (j t)", z=PASSES, h=2, j=2)[0, 0])
        nc.sync.dma_start(offsets[:], offs)
        for i in range(2, PLANES - 1):
            nc.sync.dma_start(out=planes[i][:], in_=rows[i // PACK, i % PACK])
        for lo, hi, share in STRIPS:
            nc.sync.dma_start(out=planes[-1][:, lo:hi], in_=rows[PASSES - 1, PACK - 1][:, lo:hi])
        for z in range(PASSES):
            nc.sync.dma_start(
                out=w_codes[z][:].bitcast(I32),
                in_=w1_words[z].rearrange("p c r -> p (c r)").bitcast(I32),
            )
        nc.sync.dma_start(tasks[:], task)
        nc.sync.dma_start(out=table[:], in_=scale)

        scale_rows = w1_scales.rearrange("z (q r) c -> r q z c", r=SCALE_ROWS)
        for r in range(SCALE_ROWS):
            nc.scalar.dma_start(out=w_scales[r:P:QUADRANT].bitcast(I32), in_=scale_rows[r].bitcast(I32))

        def entries(list_tile, lo, hi):
            return list_tile[:, lo // GROUP : hi // GROUP]

        grouped = [keep.tile([P, S * PACK], BF16, name="grouped%d" % z, align_bytes=64, offset=(3 + 2 * z) * STRETCH - S * PACK) for z in range(PASSES)]
        x_codes = [keep.tile([P, S], U32, name="x_codes%d" % z, align_bytes=64, offset=4 * STRETCH + 16384 + 2048 * z) for z in range(PASSES)]

        def slot(i, lo, hi):
            z, j = divmod(i, PACK)
            return grouped[z][:, lo * PACK : hi * PACK].rearrange("p (n j) -> p n j", j=PACK)[:, :, j]

        def picked(i, lo, hi, part=False):
            window = head[:, 0:T] if part else planes[i][:]
            return window.indirect(entries(offsets, lo, hi))

        def gather_staged(i, lo, hi):
            staged = keep.tile([P, hi - lo], F32 if i == 1 else BF16, name="staged%d_%d" % (i, lo), align_bytes=64, offset=4 * STRETCH + 2048 * i + 2 * lo)
            nc.vector.tensor_copy(staged[:], picked(i, lo, hi))
            return staged

        def quantise(z, lo, hi, scales):
            nc.vector.quantize_mx(
                out=x_codes[z][:, lo:hi].bitcast(FP8X4), scales=scales, in_=grouped[z][:, lo * PACK : hi * PACK]
            )

        def product(bank, z, lo, hi, scales, start, stop):
            nc.tensor.matmul_mx(
                out=bank,
                lhsT=w_codes[z][:].bitcast(FP8X4),
                lhsT_scale=w_scales[:, z, :],
                rhs=x_codes[z][:, lo:hi].bitcast(FP8X4),
                rhs_scale=scales,
                start=start,
                stop=stop,
            )

        banks = [psum.tile([N, QUARTER], F32, name="bank%d" % q) for q in range(4)]

        pair = keep.tile([P, 2, QUARTER], BF16, name="pair", align_bytes=64, offset=4 * STRETCH + 20480)
        first_scales = keep.tile([P, S], U8, name="first_scales", align_bytes=64, offset=4 * STRETCH + 21504)
        for i in range(PLANES - 1):
            width = HALF if i < PLANES - 2 else QUARTER
            for lo in range(HALF, S, width):
                staged = gather_staged(i, lo, lo + width)
                nc.scalar.copy(slot(i, lo, lo + width), staged[:])
            if i < PLANES - 2:
                nc.vector.tensor_copy(slot(i, 0, HALF), picked(i, 0, HALF, i == 0))
            else:
                staged = gather_staged(i, 0, QUARTER)
                nc.vector.tensor_copy(pair[:, 0, :], picked(i, QUARTER, HALF))
                nc.vector.tensor_copy(slot(i, 0, QUARTER), staged[:])
            if i == PACK - 1:
                for lo in (0, HALF):
                    quantise(0, lo, lo + HALF, first_scales[:, lo : lo + HALF])
                for q in range(4):
                    lo = q * QUARTER
                    product(banks[q][:], 0, lo, lo + QUARTER, first_scales[:, lo : lo + QUARTER], True, False)

        last = PLANES - 1
        narrow = keep.tile([P, T], BF16, name="narrow", align_bytes=64, offset=3 * STRETCH + 8192)
        for lo, hi, share in STRIPS:
            if share > 0:
                nc.scalar.copy(narrow[:, lo : lo + share], planes[last][:, lo : lo + share])
            if lo + share < hi:
                nc.vector.tensor_copy(narrow[:, lo + share : hi], planes[last][:, lo + share : hi])
        staged = gather_staged(last, 0, QUARTER)
        nc.vector.tensor_copy(pair[:, 1, :], picked(last, QUARTER, HALF))
        nc.vector.tensor_copy(slot(last, 0, QUARTER), staged[:])
        tokens = grouped[1][:, QUARTER * PACK : HALF * PACK].rearrange("p (n j) -> p n j", j=PACK)
        nc.vector.tensor_copy(tokens[:, :, 2:4], pair[:].rearrange("p j n -> p n j"))
        nc.scalar.activation(slot(last, HALF, S), narrow[:].indirect(entries(offsets, HALF, S)), COPY)

        for q, bank in enumerate(banks):
            lo, hi = q * QUARTER, (q + 1) * QUARTER
            scales = keep.tile([P, hi - lo], U8, name="last_scales%d" % lo, align_bytes=64, offset=4 * STRETCH + 22528 + lo)
            quantise(1, lo, hi, scales[:])
            product(bank[:], 1, lo, hi, scales[:], False, True)

        gains = keep.tile([P, S], F32, name="gains", offset=3 * STRETCH + 16384)
        result = keep.tile([N, S], F32, name="result", offset=4 * STRETCH + 24576)
        for lo, hi in SCALAR_GAINS:
            nc.scalar.activation(gains[:, lo:hi], table[:].indirect(entries(tasks, lo, hi)), COPY)
        lo, hi = VECTOR_GAINS
        nc.vector.tensor_copy(gains[:, lo:hi], table[:].indirect(entries(tasks, lo, hi)))
        for group in ((0, 1), (3,), (2,)):
            for q in group:
                cols = slice(q * QUARTER, (q + 1) * QUARTER)
                nc.vector.tensor_tensor(result[:, cols], banks[q][:], gains[:, cols], MULT)
            cols = slice(group[0] * QUARTER, (group[-1] + 1) * QUARTER)
            nc.sync.dma_start(out=out[:, cols], in_=result[:, cols])
